import numpy as np
import ml_dtypes


def mxq(x, axis, fmt="e4m3"):
    dtype, down = {"e4m3": (ml_dtypes.float8_e4m3fn, 7), "e5m2": (ml_dtypes.float8_e5m2, 14)}[fmt]
    v = np.moveaxis(np.asarray(x, np.float32).astype(ml_dtypes.bfloat16).astype(np.float64), axis, -1)
    blocks = v.reshape(v.shape[:-1] + (-1, 32))
    amax = np.abs(blocks).max(-1, keepdims=True)
    byte = np.maximum(np.where(amax > 0, np.frexp(amax)[1] - 1 + 127, 0) - down, 1)
    scale = np.exp2(byte - 127.0)
    codes = (blocks / scale).astype(np.float32).astype(dtype).astype(np.float64)
    return np.moveaxis((codes * scale).reshape(v.shape), -1, axis)


WIDE = False


def mx_kscale(k):
    if not WIDE:
        return np.ones(k)
    levels = np.array([10, -10, 5, -5, 0])
    if k % 512:
        return np.exp2(np.random.permutation(np.resize(levels, k // 32))).repeat(32)
    a = np.empty((k // 512, 16))
    for p in range(k // 512):
        a[p, :8] = np.random.permutation(np.resize(levels, 8))
        for g in range(8):
            far = levels[np.abs(levels - a[p, g]) >= 10]
            a[p, g + 8] = far[np.random.randint(len(far))]
    return np.exp2(a.ravel()).repeat(32)


def f64(x):
    return np.asarray(x).astype(np.float64)


def striped(idx):
    return np.tile(np.asarray(idx).reshape(-1, 16).T, (8, 1)).astype(np.uint16)


def unstriped(offs):
    return offs[:16].T.reshape(-1).astype(np.int64)


def striped8(idx):
    return np.asarray(idx).reshape(8, -1, 16).transpose(0, 2, 1).reshape(128, -1).astype(np.uint16)


def unstriped8(offs):
    return offs.reshape(8, 16, -1).transpose(0, 2, 1).reshape(8, -1).astype(np.int64)


def pick8(x, idx, run):
    r = np.arange(len(x))
    return x[r[:, None], idx[r % (8 * run) // run]]


E2M1 = np.array([0.0, 0.5, 1.0, 1.5, 2.0, 3.0, 4.0, 6.0, -0.0, -0.5, -1.0, -1.5, -2.0, -3.0, -4.0, -6.0])


def pack_weight(w, fmt):
    k, n = w.shape
    w = f64(np.asarray(w, np.float32).astype(ml_dtypes.bfloat16)).reshape(k // 32, 32, n)
    amax = np.abs(w).max(1)
    if fmt == "e4m3":
        byte = np.frexp(amax)[1] - 1 + 127 - 7
    else:
        mant, ex = np.frexp(amax / 6.0)
        byte = np.where(mant > 0.5, ex, ex - 1) + 127
    byte = np.clip(np.where(amax > 0, byte, 1), 1, 254)
    scaled = (w * np.exp2(127.0 - byte)[:, None, :]).reshape(k, n).astype(np.float32)
    by_word = np.ascontiguousarray(scaled.reshape(k // 512, 128, 4, n).transpose(0, 1, 3, 2))
    if fmt == "e4m3":
        words = by_word.astype(ml_dtypes.float8_e4m3fn).view(np.uint8)
    else:
        c = by_word.astype(ml_dtypes.float4_e2m1fn).view(np.uint8) & 0xF
        words = (c[..., 0::2] | (c[..., 1::2] << 4)).reshape(k // 512, 128, 2 * n)
    return np.ascontiguousarray(words), np.ascontiguousarray(byte.astype(np.uint8).reshape(k // 512, 16, n))


def unpack_weight(words, scales, fmt):
    g, _, n = scales.shape
    words = np.ascontiguousarray(words).reshape(g, 128, n, -1)
    if fmt == "e4m3":
        vals = words.view(ml_dtypes.float8_e4m3fn).astype(np.float64)
    else:
        nib = np.empty((g, 128, n, 4), np.uint8)
        nib[..., 0::2] = words & 0xF
        nib[..., 1::2] = words >> 4
        vals = E2M1[nib]
    vals = vals * np.repeat(np.exp2(scales.astype(np.float64) - 127.0), 8, axis=1)[..., None]
    return vals.transpose(0, 1, 3, 2).reshape(g * 512, n)


K, J, R, T, F, G, O, D, N = 512, 512, 512, 2048, 2048, 1024, 256, 1024, 256


def setup_inputs():
    n = np.random.standard_normal
    idx = np.random.permutation(T)[:J]
    idx2 = np.stack([np.random.permutation(F)[:R] for _ in range(8)])
    idx3 = np.stack([np.random.permutation(G)[:R] for _ in range(8)])
    idx4 = np.stack([np.random.permutation(G)[:R] for _ in range(8)])
    idx5 = np.stack([np.random.permutation(J)[:O] for _ in range(8)])
    idx6 = np.stack([np.random.permutation(D)[:O] for _ in range(8)])
    idx7 = np.random.permutation(T)[:O]
    fk = mx_kscale(K)
    fr = mx_kscale(R)
    xtp = pack_weight(n((K, T)) * fk[:, None], "e4m3")
    wbp = pack_weight(n((R, N)) * 1 / np.sqrt(R) / fr[:, None], "e2m1")
    wsp = pack_weight(n((K, N)) * 1 / np.sqrt(K) / fk[:, None], "e2m1")
    return {
        "xt_words": xtp[0],
        "xt_scales": xtp[1],
        "ua": (np.random.randint(-7, 8, (K, F)).astype(np.float64)).astype(np.float32),
        "ha": ((np.random.randint(8, 25, (K, 1)) / 1024.0) / fk[:, None]).astype(np.float32),
        "hb": (np.random.uniform(0.5, 1.6, (K, 1))).astype(np.float32),
        "tl": (np.random.randint(-7, 8, (R, D)).astype(np.float64)).astype(np.float32),
        "sa": (np.random.uniform(0.5, 1.6, (R, 1)) * fr[:, None]).astype(np.float32),
        "sl": ((np.random.randint(6, 19, (R, 1)) / 64.0) * fr[:, None]).astype(np.float32),
        "wb_words": wbp[0],
        "wb_scales": wbp[1],
        "ws_words": wsp[0],
        "ws_scales": wsp[1],
        "offs": striped(idx),
        "offs2": striped8(idx2),
        "offs3": striped8(idx3),
        "offs4": striped8(idx4),
        "offs5": striped8(idx5),
        "offs6": striped8(idx6),
        "offs7": striped(idx7),
    }


def reference(xt_words, xt_scales, ua, ha, hb, tl, sa, sl, wb_words, wb_scales, ws_words, ws_scales, offs, offs2, offs3, offs4, offs5, offs6, offs7):
    idx = unstriped(offs)
    idx2 = unstriped8(offs2)
    idx3 = unstriped8(offs3)
    idx4 = unstriped8(offs4)
    idx5 = unstriped8(offs5)
    idx6 = unstriped8(offs6)
    idx7 = unstriped(offs7)
    xtu = unpack_weight(xt_words, xt_scales, "e4m3")
    wbu = unpack_weight(wb_words, wb_scales, "e2m1")
    wsu = unpack_weight(ws_words, ws_scales, "e2m1")
    wcd = pick8(f64(ua), idx2, 64) * f64(ha)
    wcp = np.zeros((K, G))
    wcp[np.arange(K)[:, None], idx3[np.arange(K) % 512 // 64]] = wcd
    wc = pick8(wcp, idx4, 64) * f64(hb)
    wcq = mxq(wc, 0, "e4m3")
    xtidxg = xtu[:, idx]
    a = wcq.T @ xtidxg
    hid = np.maximum(pick8(a, idx5, 64) * f64(sa), pick8(f64(tl), idx6, 64) * f64(sl))
    hidq = mxq(hid, 0, "e4m3")
    xtidx7g = xtu[:, idx7]
    y = wbu.T @ hidq + wsu.T @ xtidx7g
    return y

@@ -1,0 +1,191 @@
+from contextlib import ExitStack
+
+import concourse.mybir as mybir
+
+K, J, R, T, F, G, O, D, N = 512, 512, 512, 2048, 2048, 1024, 256, 1024, 256
+FLOPS = 2 * (K * R * J + R * N * O + K * N * O)
+
+F32 = mybir.dt.float32
+BF16 = mybir.dt.bfloat16
+I32 = mybir.dt.int32
+U32 = mybir.dt.uint32
+U16 = mybir.dt.uint16
+U8 = mybir.dt.uint8
+FP8X4 = mybir.dt.float8_e4m3fn_x4
+FP4X4 = mybir.dt.float4_e2m1fn_x4
+COPY = mybir.ActivationFunctionType.Copy
+MAX = mybir.AluOpType.max
+
+P = 128
+PACK = 4
+HALF = O // 2
+
+
+def tile_picked_tokens_codepage_one_codedlevel_further_plain_kernel(
+    tc, xt_words, xt_scales, ua, ha, hb, tl, sa, sl, wb_words, wb_scales, ws_words, ws_scales,
+    offs, offs2, offs3, offs4, offs5, offs6, offs7, out,
+):
+    nc = tc.nc
+    with ExitStack() as ctx:
+        lists = ctx.enter_context(tc.tile_pool(name="lists", bufs=1))
+        sb = ctx.enter_context(tc.tile_pool(name="sb", bufs=1))
+        psum = ctx.enter_context(tc.psum_pool(name="psum", bufs=1))
+
+        def tile(shape, dtype, name, tag=None):
+            return sb.tile(shape, dtype, name=name, tag=tag or name, align_bytes=64)
+
+        def load_list(src, name):
+            dst = lists.tile(list(src.shape), U16, name=name)
+            nc.sync.dma_start(dst[:], src)
+            return dst
+
+        def load_factors(queue, src, name):
+            dst = tile([P, PACK], F32, name)
+            queue.dma_start(dst[:], src.rearrange("(p t) one -> p (t one)", t=PACK))
+            return dst
+
+        def load_rows(src, t, name):
+            dst = tile([P, src.shape[1]], F32, name)
+            nc.sync.dma_start(dst[:], src.rearrange("(p t) c -> t p c", t=PACK)[t])
+            return dst
+
+        def cleared_scales(width, name):
+            dst = tile([P, width], U8, name)
+            nc.vector.memset(dst[:].bitcast(I32), 0)
+            return dst
+
+        def load_scales(queue, dst, src):
+            for q in range(4):
+                queue.dma_start(dst[32 * q : 32 * q + 4, :].bitcast(I32), src[0, 4 * q : 4 * q + 4, :].bitcast(I32))
+
+        def load_fp4(src, name):
+            dst = tile([P, 2 * N], U8, name)
+            nc.sync.dma_start(dst[:].bitcast(I32), src[0].bitcast(I32))
+            return dst
+
+        xt_s = cleared_scales(T, "xt_s")
+        pages = []
+        for t in range(PACK):
+            page = tile([P, G], F32, f"page{t}")
+            nc.vector.memset(page[:].bitcast(I32), 0)
+            pages.append(page)
+        wb_s = cleared_scales(N, "wb_s")
+        ws_s = cleared_scales(N, "ws_s")
+
+        l2 = load_list(offs2, "l2")
+        ha_t = load_factors(nc.scalar, ha, "ha_t")
+        ua_t = [load_rows(ua, 0, "ua0")]
+        load_scales(nc.scalar, xt_s, xt_scales)
+        l1 = load_list(offs, "l1")
+        l3 = load_list(offs3, "l3")
+        ua_t.append(load_rows(ua, 1, "ua1"))
+        l7 = load_list(offs7, "l7")
+        hb_t = load_factors(nc.sync, hb, "hb_t")
+        l4 = load_list(offs4, "l4")
+        ua_t.append(load_rows(ua, 2, "ua2"))
+        l6 = load_list(offs6, "l6")
+        sl_t = load_factors(nc.sync, sl, "sl_t")
+        tl_t = [load_rows(tl, u, f"tl{u}") for u in range(1)]
+        ua_t.append(load_rows(ua, 3, "ua3"))
+        xt_w = tile([P, T], I32, "xt_w")
+        nc.sync.dma_start(xt_w[:], xt_words[0].rearrange("p c t -> p (c t)").bitcast(I32))
+        tl_t.extend([load_rows(tl, u, f"tl{u}") for u in range(1, PACK)])
+        l5 = load_list(offs5, "l5")
+        sa_t = load_factors(nc.sync, sa, "sa_t")
+        ws_w = load_fp4(ws_words, "ws_w")
+        wb_w = load_fp4(wb_words, "wb_w")
+        load_scales(nc.sync, ws_s, ws_scales)
+        load_scales(nc.sync, wb_s, wb_scales)
+
+        x1_s = tile([P, J], U8, "x1_s")
+        nc.vector.tensor_copy(x1_s[:], xt_s[:].indirect(l1[:]))
+
+        for t in range(PACK):
+            wcd = tile([P, R], F32, f"wcd{t}")
+            nc.scalar.activation(wcd[:], ua_t[t][:].indirect(l2[:]), COPY, scale=ha_t[:, t : t + 1])
+            nc.vector.tensor_copy(pages[t][:].indirect(l3[:]), wcd[:])
+
+        wc = tile([P, PACK, R], BF16, "wc", tag="ua3")
+        for t in range(PACK):
+            nc.scalar.activation(wc[:, t, :], pages[t][:].indirect(l4[:]), COPY, scale=hb_t[:, t : t + 1])
+
+        x1_w = tile([P, J], U32, "x1_w", tag="wcd3")
+        nc.vector.tensor_copy(x1_w[:], xt_w[:].bitcast(U32).indirect(l1[:]))
+
+        level = tile([P, PACK, O], F32, "level")
+        for u in range(PACK):
+            nc.scalar.activation(level[:, u, :], tl_t[u][:].indirect(l6[:]), COPY, scale=sl_t[:, u : u + 1])
+
+        wc_dealt = wc[:].rearrange("p t (m u) -> p u m t", u=PACK)
+        grouped = [tile([P, P, PACK], BF16, f"grouped{u}") for u in range(PACK)]
+        codes = [tile([P, P], U32, f"wc_w{u}") for u in range(PACK)]
+        scales = [tile([P, P], U8, f"wc_s{u}") for u in range(PACK)]
+        a_t = [tile([P, J], F32, f"a{u}") for u in range(PACK)]
+
+        def interleave(u):
+            nc.vector.tensor_copy(grouped[u][:], wc_dealt[:, u])
+
+        def multiply(u):
+            nc.vector.quantize_mx(codes[u][:].bitcast(FP8X4), scales[u][:], grouped[u][:].rearrange("p m t -> p (m t)"))
+            acc = psum.tile([P, J], F32, name=f"acc{u}")
+            nc.tensor.matmul_mx(acc[:], lhsT=codes[u][:].bitcast(FP8X4), lhsT_scale=scales[u][:],
+                                rhs=x1_w[:].bitcast(FP8X4), rhs_scale=x1_s[:], start=True, stop=True)
+            return acc
+
+        accs = []
+        interleave(0)
+        for u in range(PACK):
+            if u + 1 < PACK:
+                interleave(u + 1)
+            accs.append(multiply(u))
+        nc.scalar.copy(a_t[0][:], accs[0][:])
+        for u in range(1, PACK):
+            nc.vector.tensor_copy(a_t[u][:], accs[u][:])
+
+        x7_w = tile([P, O], U32, "x7_w", tag="wc_w3")
+        nc.vector.tensor_copy(x7_w[:], xt_w[:].bitcast(U32).indirect(l7[:]))
+
+        x7_s = tile([P, O], U8, "x7_s", tag="wc_s3")
+        nc.vector.tensor_copy(x7_s[:], xt_s[:].indirect(l7[:]))
+
+        def fp4_pass(acc, words, planes, b, rhs, rhs_scale, first):
+            nc.tensor.matmul_mx(acc[:], lhsT=words[:, 2 * P * b : 2 * P * (b + 1)].bitcast(FP4X4),
+                                lhsT_scale=planes[:, P * b : P * (b + 1)], rhs=rhs.bitcast(FP8X4),
+                                rhs_scale=rhs_scale, start=first, stop=not first)
+
+        blocks = N // P
+        out_v = out.rearrange("(b p) o -> p b o", p=P)
+        picked = []
+        for h in range(2):
+            got = tile([P, PACK, HALF], F32, f"picked{h}")
+            for u in range(PACK):
+                nc.scalar.activation(got[:, u, :], a_t[u][:].indirect(l5[:, h * HALF // 16 : (h + 1) * HALF // 16]),
+                                     COPY, scale=sa_t[:, u : u + 1])
+            picked.append(got)
+        hid = []
+        for h in range(2):
+            cols = slice(h * HALF, (h + 1) * HALF)
+            both = tile([P, HALF, PACK], BF16, f"hid{h}")
+            nc.vector.tensor_tensor(both[:].rearrange("p (c i) u -> p c u i", i=4),
+                                    picked[h][:].rearrange("p u (c i) -> p c u i", i=4),
+                                    level[:, :, cols].rearrange("p u (c i) -> p c u i", i=4), MAX)
+            hid.append(both)
+        ys = [[psum.tile([P, HALF], F32, name=f"y{h}{b}") for b in range(blocks)] for h in range(2)]
+        for h in range(2):
+            cols = slice(h * HALF, (h + 1) * HALF)
+            for b in range(blocks):
+                fp4_pass(ys[h][b], ws_w, ws_s, b, x7_w[:, cols], x7_s[:, cols], True)
+        for h in range(2):
+            cols = slice(h * HALF, (h + 1) * HALF)
+            hid_w = tile([P, HALF], U32, f"hid_w{h}")
+            hid_s = tile([P, HALF], U8, f"hid_s{h}")
+            nc.vector.quantize_mx(hid_w[:].bitcast(FP8X4), hid_s[:], hid[h][:].rearrange("p o u -> p (o u)"))
+            res = tile([P, blocks, HALF], F32, f"res{h}")
+            for b in range(blocks):
+                fp4_pass(ys[h][b], wb_w, wb_s, b, hid_w[:], hid_s[:], False)
+            nc.scalar.copy(res[:, 0, :], ys[h][0][:])
+            if h == 0:
+                nc.scalar.copy(res[:, 1, :], ys[h][1][:])
+            else:
+                nc.vector.tensor_copy(res[:, 1, :], ys[h][1][:])
+            nc.sync.dma_start(out_v[:, :, cols], res[:])

@@ -64,6 +64,8 @@ def tile_picked_tokens_codepage_one_codedlevel_further_plain_kernel(
             return dst
 
         xt_s = cleared_scales(T, "xt_s")
+        warm_in = tile([P, 1], F32, "warm_in")
+        nc.vector.memset(warm_in[:], 0.0)
         pages = []
         for t in range(PACK):
             page = tile([P, G], F32, f"page{t}")
@@ -76,6 +78,8 @@ def tile_picked_tokens_codepage_one_codedlevel_further_plain_kernel(
         ha_t = load_factors(nc.scalar, ha, "ha_t")
         ua_t = [load_rows(ua, 0, "ua0")]
         load_scales(nc.scalar, xt_s, xt_scales)
+        warm_out = tile([P, 1], F32, "warm_out")
+        nc.scalar.activation(warm_out[:], warm_in[:], COPY)
         l1 = load_list(offs, "l1")
         l3 = load_list(offs3, "l3")
         ua_t.append(load_rows(ua, 1, "ua1"))

@@ -44,6 +44,12 @@ def tile_picked_tokens_codepage_one_codedlevel_further_plain_kernel(
             queue.dma_start(dst[:], src.rearrange("(p t) one -> p (t one)", t=PACK))
             return dst
 
+        def load_factor_columns(src, t0, t1):
+            dst = tile([P, t1 - t0], F32, f"hb{t0}")
+            with nc.allow_non_contiguous_dma(reason="one value a partition"):
+                nc.sync.dma_start(dst[:], src.rearrange("(p t) one -> p (t one)", t=PACK)[:, t0:t1])
+            return [dst[:, t : t + 1] for t in range(t1 - t0)]
+
         def load_rows(src, t, name):
             dst = tile([P, src.shape[1]], F32, name)
             nc.sync.dma_start(dst[:], src.rearrange("(p t) c -> t p c", t=PACK)[t])
@@ -71,29 +77,40 @@ def tile_picked_tokens_codepage_one_codedlevel_further_plain_kernel(
             page = tile([P, G], F32, f"page{t}")
             nc.vector.memset(page[:].bitcast(I32), 0)
             pages.append(page)
+        x_s = cleared_scales(J + O, "x_s")
         wb_s = cleared_scales(N, "wb_s")
         ws_s = cleared_scales(N, "ws_s")
 
         l2 = load_list(offs2, "l2")
+        l7 = load_list(offs7, "l7")
         ha_t = load_factors(nc.scalar, ha, "ha_t")
         ua_t = [load_rows(ua, 0, "ua0")]
-        load_scales(nc.scalar, xt_s, xt_scales)
+        nc.scalar.dma_start(xt_s[0:P:8, :].bitcast(I32), xt_scales[0].bitcast(I32))
         warm_out = tile([P, 1], F32, "warm_out")
         nc.scalar.activation(warm_out[:], warm_in[:], COPY)
         l1 = load_list(offs, "l1")
         l3 = load_list(offs3, "l3")
-        ua_t.append(load_rows(ua, 1, "ua1"))
-        l7 = load_list(offs7, "l7")
-        hb_t = load_factors(nc.sync, hb, "hb_t")
         l4 = load_list(offs4, "l4")
-        ua_t.append(load_rows(ua, 2, "ua2"))
         l6 = load_list(offs6, "l6")
+        ua_t.append(load_rows(ua, 1, "ua1"))
         sl_t = load_factors(nc.sync, sl, "sl_t")
-        tl_t = [load_rows(tl, u, f"tl{u}") for u in range(1)]
+        tl_t = [load_rows(tl, 0, "tl0")]
+        hb_cols = load_factor_columns(hb, 0, 1)
+        ua_t.append(load_rows(ua, 2, "ua2"))
         ua_t.append(load_rows(ua, 3, "ua3"))
+        hb_cols.extend(load_factor_columns(hb, 1, 3))
+        tl_t.extend([load_rows(tl, u, f"tl{u}") for u in range(1, PACK)])
         xt_w = tile([P, T], I32, "xt_w")
         nc.sync.dma_start(xt_w[:], xt_words[0].rearrange("p c t -> p (c t)").bitcast(I32))
-        tl_t.extend([load_rows(tl, u, f"tl{u}") for u in range(1, PACK)])
+        hb_cols.extend(load_factor_columns(hb, 3, 4))
+
+        got_s = tile([P, J + O], U8, "got_s")
+        nc.vector.tensor_copy(got_s[:, J:], xt_s[:].indirect(l7[:]))
+        nc.vector.tensor_copy(got_s[:, :J], xt_s[:].indirect(l1[:]))
+        for q in range(4):
+            nc.sync.dma_start(x_s[32 * q : 32 * q + 4, :].bitcast(I32), got_s[32 * q : 32 * q + 32 : 8, :].bitcast(I32))
+        x1_s, x7_s = x_s[:, :J], x_s[:, J:]
+
         l5 = load_list(offs5, "l5")
         sa_t = load_factors(nc.sync, sa, "sa_t")
         ws_w = load_fp4(ws_words, "ws_w")
@@ -101,24 +118,21 @@ def tile_picked_tokens_codepage_one_codedlevel_further_plain_kernel(
         load_scales(nc.sync, ws_s, ws_scales)
         load_scales(nc.sync, wb_s, wb_scales)
 
-        x1_s = tile([P, J], U8, "x1_s")
-        nc.vector.tensor_copy(x1_s[:], xt_s[:].indirect(l1[:]))
-
         for t in range(PACK):
             wcd = tile([P, R], F32, f"wcd{t}")
             nc.scalar.activation(wcd[:], ua_t[t][:].indirect(l2[:]), COPY, scale=ha_t[:, t : t + 1])
             nc.vector.tensor_copy(pages[t][:].indirect(l3[:]), wcd[:])
 
-        wc = tile([P, PACK, R], BF16, "wc", tag="ua3")
-        for t in range(PACK):
-            nc.scalar.activation(wc[:, t, :], pages[t][:].indirect(l4[:]), COPY, scale=hb_t[:, t : t + 1])
-
-        x1_w = tile([P, J], U32, "x1_w", tag="wcd3")
-        nc.vector.tensor_copy(x1_w[:], xt_w[:].bitcast(U32).indirect(l1[:]))
-
         level = tile([P, PACK, O], F32, "level")
         for u in range(PACK):
             nc.scalar.activation(level[:, u, :], tl_t[u][:].indirect(l6[:]), COPY, scale=sl_t[:, u : u + 1])
+
+        wc = tile([P, PACK, R], BF16, "wc")
+        for t in range(PACK):
+            nc.scalar.activation(wc[:, t, :], pages[t][:].indirect(l4[:]), COPY, scale=hb_cols[t])
+
+        x1_w = tile([P, J], U32, "x1_w", tag="wcd3")
+        nc.vector.tensor_copy(x1_w[:], xt_w[:].bitcast(U32).indirect(l1[:]))
 
         wc_dealt = wc[:].rearrange("p t (m u) -> p u m t", u=PACK)
         grouped = [tile([P, P, PACK], BF16, f"grouped{u}") for u in range(PACK)]
@@ -127,14 +141,23 @@ def tile_picked_tokens_codepage_one_codedlevel_further_plain_kernel(
         a_t = [tile([P, J], F32, f"a{u}") for u in range(PACK)]
 
         def interleave(u):
-            nc.vector.tensor_copy(grouped[u][:], wc_dealt[:, u])
+            if u < 2:
+                nc.vector.tensor_copy(grouped[u][:], wc_dealt[:, u])
+            else:
+                nc.scalar.copy(grouped[u][:], wc_dealt[:, u])
 
         def multiply(u):
             nc.vector.quantize_mx(codes[u][:].bitcast(FP8X4), scales[u][:], grouped[u][:].rearrange("p m t -> p (m t)"))
-            acc = psum.tile([P, J], F32, name=f"acc{u}")
-            nc.tensor.matmul_mx(acc[:], lhsT=codes[u][:].bitcast(FP8X4), lhsT_scale=scales[u][:],
-                                rhs=x1_w[:].bitcast(FP8X4), rhs_scale=x1_s[:], start=True, stop=True)
-            return acc
+            parts = 2 if u == 0 else 1
+            width = J // parts
+            banks = []
+            for k in range(parts):
+                cols = slice(k * width, (k + 1) * width)
+                acc = psum.tile([P, width], F32, name=f"acc{u}{k}")
+                nc.tensor.matmul_mx(acc[:], lhsT=codes[u][:].bitcast(FP8X4), lhsT_scale=scales[u][:],
+                                    rhs=x1_w[:, cols].bitcast(FP8X4), rhs_scale=x1_s[:, cols], start=True, stop=True)
+                banks.append(acc)
+            return banks
 
         accs = []
         interleave(0)
@@ -142,15 +165,14 @@ def tile_picked_tokens_codepage_one_codedlevel_further_plain_kernel(
             if u + 1 < PACK:
                 interleave(u + 1)
             accs.append(multiply(u))
-        nc.scalar.copy(a_t[0][:], accs[0][:])
+            if u == 0:
+                nc.scalar.copy(a_t[0][:, : J // 2], accs[0][0][:])
+                nc.vector.tensor_copy(a_t[0][:, J // 2 :], accs[0][1][:])
         for u in range(1, PACK):
-            nc.vector.tensor_copy(a_t[u][:], accs[u][:])
+            nc.vector.tensor_copy(a_t[u][:], accs[u][0][:])
 
         x7_w = tile([P, O], U32, "x7_w", tag="wc_w3")
         nc.vector.tensor_copy(x7_w[:], xt_w[:].bitcast(U32).indirect(l7[:]))
-
-        x7_s = tile([P, O], U8, "x7_s", tag="wc_s3")
-        nc.vector.tensor_copy(x7_s[:], xt_s[:].indirect(l7[:]))
 
         def fp4_pass(acc, words, planes, b, rhs, rhs_scale, first):
             nc.tensor.matmul_mx(acc[:], lhsT=words[:, 2 * P * b : 2 * P * (b + 1)].bitcast(FP4X4),
@@ -159,22 +181,22 @@ def tile_picked_tokens_codepage_one_codedlevel_further_plain_kernel(
 
         blocks = N // P
         out_v = out.rearrange("(b p) o -> p b o", p=P)
-        picked = []
+        picked = tile([P, PACK, O], F32, "picked")
+        for u in range(PACK - 1):
+            nc.scalar.activation(picked[:, u, :], a_t[u][:].indirect(l5[:]), COPY, scale=sa_t[:, u : u + 1])
         for h in range(2):
-            got = tile([P, PACK, HALF], F32, f"picked{h}")
-            for u in range(PACK):
-                nc.scalar.activation(got[:, u, :], a_t[u][:].indirect(l5[:, h * HALF // 16 : (h + 1) * HALF // 16]),
-                                     COPY, scale=sa_t[:, u : u + 1])
-            picked.append(got)
+            nc.scalar.activation(picked[:, 3, h * HALF : (h + 1) * HALF],
+                                 a_t[3][:].indirect(l5[:, h * HALF // 16 : (h + 1) * HALF // 16]),
+                                 COPY, scale=sa_t[:, 3:4])
         hid = []
         for h in range(2):
             cols = slice(h * HALF, (h + 1) * HALF)
             both = tile([P, HALF, PACK], BF16, f"hid{h}")
             nc.vector.tensor_tensor(both[:].rearrange("p (c i) u -> p c u i", i=4),
-                                    picked[h][:].rearrange("p u (c i) -> p c u i", i=4),
+                                    picked[:, :, cols].rearrange("p u (c i) -> p c u i", i=4),
                                     level[:, :, cols].rearrange("p u (c i) -> p c u i", i=4), MAX)
             hid.append(both)
-        ys = [[psum.tile([P, HALF], F32, name=f"y{h}{b}") for b in range(blocks)] for h in range(2)]
+        ys = [[psum.tile([P, HALF], F32, name=f"y{h}{b}", tag=("acc00" if h + b == 2 else f"y{h}{b}")) for b in range(blocks)] for h in range(2)]
         for h in range(2):
             cols = slice(h * HALF, (h + 1) * HALF)
             for b in range(blocks):
@@ -184,12 +206,17 @@ def tile_picked_tokens_codepage_one_codedlevel_further_plain_kernel(
             hid_w = tile([P, HALF], U32, f"hid_w{h}")
             hid_s = tile([P, HALF], U8, f"hid_s{h}")
             nc.vector.quantize_mx(hid_w[:].bitcast(FP8X4), hid_s[:], hid[h][:].rearrange("p o u -> p (o u)"))
-            res = tile([P, blocks, HALF], F32, f"res{h}")
             for b in range(blocks):
                 fp4_pass(ys[h][b], wb_w, wb_s, b, hid_w[:], hid_s[:], False)
-            nc.scalar.copy(res[:, 0, :], ys[h][0][:])
             if h == 0:
-                nc.scalar.copy(res[:, 1, :], ys[h][1][:])
+                res = tile([P, blocks, HALF], F32, "res0")
+                for b in range(blocks):
+                    nc.scalar.copy(res[:, b, :], ys[h][b][:])
+                nc.sync.dma_start(out_v[:, :, cols], res[:])
             else:
-                nc.vector.tensor_copy(res[:, 1, :], ys[h][1][:])
-            nc.sync.dma_start(out_v[:, :, cols], res[:])
+                res_a = tile([P, HALF], F32, "res10")
+                nc.scalar.copy(res_a[:], ys[h][0][:])
+                nc.scalar.dma_start(out_v[:, 0, cols], res_a[:])
+                res_b = tile([P, HALF], F32, "res11")
+                nc.vector.tensor_copy(res_b[:], ys[h][1][:])
+                nc.sync.dma_start(out_v[:, 1, cols], res_b[:])

from contextlib import ExitStack

import concourse.mybir as mybir

K, J, R, T, F, G, O, D, N = 512, 512, 512, 2048, 2048, 1024, 256, 1024, 256
FLOPS = 2 * (K * R * J + R * N * O + K * N * O)

F32 = mybir.dt.float32
BF16 = mybir.dt.bfloat16
I32 = mybir.dt.int32
U32 = mybir.dt.uint32
U16 = mybir.dt.uint16
U8 = mybir.dt.uint8
FP8X4 = mybir.dt.float8_e4m3fn_x4
FP4X4 = mybir.dt.float4_e2m1fn_x4
COPY = mybir.ActivationFunctionType.Copy
MAX = mybir.AluOpType.max

P = 128
PACK = 4
HALF = O // 2


def tile_picked_tokens_codepage_one_codedlevel_further_plain_kernel(
    tc, xt_words, xt_scales, ua, ha, hb, tl, sa, sl, wb_words, wb_scales, ws_words, ws_scales,
    offs, offs2, offs3, offs4, offs5, offs6, offs7, out,
):
    nc = tc.nc
    with ExitStack() as ctx:
        lists = ctx.enter_context(tc.tile_pool(name="lists", bufs=1))
        sb = ctx.enter_context(tc.tile_pool(name="sb", bufs=1))
        psum = ctx.enter_context(tc.psum_pool(name="psum", bufs=1))

        def tile(shape, dtype, name, tag=None):
            return sb.tile(shape, dtype, name=name, tag=tag or name, align_bytes=64)

        def load_list(src, name):
            dst = lists.tile(list(src.shape), U16, name=name)
            nc.sync.dma_start(dst[:], src)
            return dst

        def load_factors(queue, src, name):
            dst = tile([P, PACK], F32, name)
            queue.dma_start(dst[:], src.rearrange("(p t) one -> p (t one)", t=PACK))
            return dst

        def load_factor_columns(src, t0, t1):
            dst = tile([P, t1 - t0], F32, f"hb{t0}")
            with nc.allow_non_contiguous_dma(reason="one value a partition"):
                nc.sync.dma_start(dst[:], src.rearrange("(p t) one -> p (t one)", t=PACK)[:, t0:t1])
            return [dst[:, t : t + 1] for t in range(t1 - t0)]

        def load_rows(src, t, name):
            dst = tile([P, src.shape[1]], F32, name)
            nc.sync.dma_start(dst[:], src.rearrange("(p t) c -> t p c", t=PACK)[t])
            return dst

        def cleared_scales(width, name):
            dst = tile([P, width], U8, name)
            nc.vector.memset(dst[:].bitcast(I32), 0)
            return dst

        def load_scales(queue, dst, src):
            for q in range(4):
                queue.dma_start(dst[32 * q : 32 * q + 4, :].bitcast(I32), src[0, 4 * q : 4 * q + 4, :].bitcast(I32))

        def load_fp4(src, name):
            dst = tile([P, 2 * N], U8, name)
            nc.sync.dma_start(dst[:].bitcast(I32), src[0].bitcast(I32))
            return dst

        xt_s = cleared_scales(T, "xt_s")
        warm_in = tile([P, 1], F32, "warm_in")
        nc.vector.memset(warm_in[:], 0.0)
        pages = []
        for t in range(PACK):
            page = tile([P, G], F32, f"page{t}")
            nc.vector.memset(page[:].bitcast(I32), 0)
            pages.append(page)
        x_s = cleared_scales(J + O, "x_s")
        wb_s = cleared_scales(N, "wb_s")
        ws_s = cleared_scales(N, "ws_s")

        l2 = load_list(offs2, "l2")
        l7 = load_list(offs7, "l7")
        ha_t = load_factors(nc.scalar, ha, "ha_t")
        ua_t = [load_rows(ua, 0, "ua0")]
        nc.scalar.dma_start(xt_s[0:P:8, :].bitcast(I32), xt_scales[0].bitcast(I32))
        warm_out = tile([P, 1], F32, "warm_out")
        nc.scalar.activation(warm_out[:], warm_in[:], COPY)
        l1 = load_list(offs, "l1")
        l3 = load_list(offs3, "l3")
        l4 = load_list(offs4, "l4")
        l6 = load_list(offs6, "l6")
        ua_t.append(load_rows(ua, 1, "ua1"))
        sl_t = load_factors(nc.sync, sl, "sl_t")
        tl_t = [load_rows(tl, 0, "tl0")]
        hb_cols = load_factor_columns(hb, 0, 1)
        ua_t.append(load_rows(ua, 2, "ua2"))
        ua_t.append(load_rows(ua, 3, "ua3"))
        hb_cols.extend(load_factor_columns(hb, 1, 3))
        tl_t.extend([load_rows(tl, u, f"tl{u}") for u in range(1, PACK)])
        xt_w = tile([P, T], I32, "xt_w")
        nc.sync.dma_start(xt_w[:], xt_words[0].rearrange("p c t -> p (c t)").bitcast(I32))
        hb_cols.extend(load_factor_columns(hb, 3, 4))

        got_s = tile([P, J + O], U8, "got_s")
        nc.vector.tensor_copy(got_s[:, J:], xt_s[:].indirect(l7[:]))
        nc.vector.tensor_copy(got_s[:, :J], xt_s[:].indirect(l1[:]))
        for q in range(4):
            nc.sync.dma_start(x_s[32 * q : 32 * q + 4, :].bitcast(I32), got_s[32 * q : 32 * q + 32 : 8, :].bitcast(I32))
        x1_s, x7_s = x_s[:, :J], x_s[:, J:]

        l5 = load_list(offs5, "l5")
        sa_t = load_factors(nc.sync, sa, "sa_t")
        ws_w = load_fp4(ws_words, "ws_w")
        wb_w = load_fp4(wb_words, "wb_w")
        load_scales(nc.sync, ws_s, ws_scales)
        load_scales(nc.sync, wb_s, wb_scales)

        for t in range(PACK):
            wcd = tile([P, R], F32, f"wcd{t}")
            nc.scalar.activation(wcd[:], ua_t[t][:].indirect(l2[:]), COPY, scale=ha_t[:, t : t + 1])
            nc.vector.tensor_copy(pages[t][:].indirect(l3[:]), wcd[:])

        level = tile([P, PACK, O], F32, "level")
        for u in range(PACK):
            nc.scalar.activation(level[:, u, :], tl_t[u][:].indirect(l6[:]), COPY, scale=sl_t[:, u : u + 1])

        wc = tile([P, PACK, R], BF16, "wc")
        for t in range(PACK):
            nc.scalar.activation(wc[:, t, :], pages[t][:].indirect(l4[:]), COPY, scale=hb_cols[t])

        x1_w = tile([P, J], U32, "x1_w", tag="wcd3")
        nc.vector.tensor_copy(x1_w[:], xt_w[:].bitcast(U32).indirect(l1[:]))

        wc_dealt = wc[:].rearrange("p t (m u) -> p u m t", u=PACK)
        grouped = [tile([P, P, PACK], BF16, f"grouped{u}") for u in range(PACK)]
        codes = [tile([P, P], U32, f"wc_w{u}") for u in range(PACK)]
        scales = [tile([P, P], U8, f"wc_s{u}") for u in range(PACK)]
        a_t = [tile([P, J], F32, f"a{u}") for u in range(PACK)]

        def interleave(u):
            if u < 2:
                nc.vector.tensor_copy(grouped[u][:], wc_dealt[:, u])
            else:
                nc.scalar.copy(grouped[u][:], wc_dealt[:, u])

        def multiply(u):
            nc.vector.quantize_mx(codes[u][:].bitcast(FP8X4), scales[u][:], grouped[u][:].rearrange("p m t -> p (m t)"))
            parts = 2 if u == 0 else 1
            width = J // parts
            banks = []
            for k in range(parts):
                cols = slice(k * width, (k + 1) * width)
                acc = psum.tile([P, width], F32, name=f"acc{u}{k}")
                nc.tensor.matmul_mx(acc[:], lhsT=codes[u][:].bitcast(FP8X4), lhsT_scale=scales[u][:],
                                    rhs=x1_w[:, cols].bitcast(FP8X4), rhs_scale=x1_s[:, cols], start=True, stop=True)
                banks.append(acc)
            return banks

        accs = []
        interleave(0)
        for u in range(PACK):
            if u + 1 < PACK:
                interleave(u + 1)
            accs.append(multiply(u))
            if u == 0:
                nc.scalar.copy(a_t[0][:, : J // 2], accs[0][0][:])
                nc.vector.tensor_copy(a_t[0][:, J // 2 :], accs[0][1][:])
        for u in range(1, PACK):
            nc.vector.tensor_copy(a_t[u][:], accs[u][0][:])

        x7_w = tile([P, O], U32, "x7_w", tag="wc_w3")
        nc.vector.tensor_copy(x7_w[:], xt_w[:].bitcast(U32).indirect(l7[:]))

        def fp4_pass(acc, words, planes, b, rhs, rhs_scale, first):
            nc.tensor.matmul_mx(acc[:], lhsT=words[:, 2 * P * b : 2 * P * (b + 1)].bitcast(FP4X4),
                                lhsT_scale=planes[:, P * b : P * (b + 1)], rhs=rhs.bitcast(FP8X4),
                                rhs_scale=rhs_scale, start=first, stop=not first)

        blocks = N // P
        out_v = out.rearrange("(b p) o -> p b o", p=P)
        picked = tile([P, PACK, O], F32, "picked")
        for u in range(PACK - 1):
            nc.scalar.activation(picked[:, u, :], a_t[u][:].indirect(l5[:]), COPY, scale=sa_t[:, u : u + 1])
        for h in range(2):
            nc.scalar.activation(picked[:, 3, h * HALF : (h + 1) * HALF],
                                 a_t[3][:].indirect(l5[:, h * HALF // 16 : (h + 1) * HALF // 16]),
                                 COPY, scale=sa_t[:, 3:4])
        hid = []
        for h in range(2):
            cols = slice(h * HALF, (h + 1) * HALF)
            both = tile([P, HALF, PACK], BF16, f"hid{h}")
            nc.vector.tensor_tensor(both[:].rearrange("p (c i) u -> p c u i", i=4),
                                    picked[:, :, cols].rearrange("p u (c i) -> p c u i", i=4),
                                    level[:, :, cols].rearrange("p u (c i) -> p c u i", i=4), MAX)
            hid.append(both)
        ys = [[psum.tile([P, HALF], F32, name=f"y{h}{b}", tag=("acc00" if h + b == 2 else f"y{h}{b}")) for b in range(blocks)] for h in range(2)]
        for h in range(2):
            cols = slice(h * HALF, (h + 1) * HALF)
            for b in range(blocks):
                fp4_pass(ys[h][b], ws_w, ws_s, b, x7_w[:, cols], x7_s[:, cols], True)
        for h in range(2):
            cols = slice(h * HALF, (h + 1) * HALF)
            hid_w = tile([P, HALF], U32, f"hid_w{h}")
            hid_s = tile([P, HALF], U8, f"hid_s{h}")
            nc.vector.quantize_mx(hid_w[:].bitcast(FP8X4), hid_s[:], hid[h][:].rearrange("p o u -> p (o u)"))
            for b in range(blocks):
                fp4_pass(ys[h][b], wb_w, wb_s, b, hid_w[:], hid_s[:], False)
            if h == 0:
                res = tile([P, blocks, HALF], F32, "res0")
                for b in range(blocks):
                    nc.scalar.copy(res[:, b, :], ys[h][b][:])
                nc.sync.dma_start(out_v[:, :, cols], res[:])
            else:
                res_a = tile([P, HALF], F32, "res10")
                nc.scalar.copy(res_a[:], ys[h][0][:])
                nc.scalar.dma_start(out_v[:, 0, cols], res_a[:])
                res_b = tile([P, HALF], F32, "res11")
                nc.vector.tensor_copy(res_b[:], ys[h][1][:])
                nc.sync.dma_start(out_v[:, 1, cols], res_b[:])
